import numpy as np
import ml_dtypes


def mxq(x, axis, fmt="e4m3"):
    dtype, down = {"e4m3": (ml_dtypes.float8_e4m3fn, 7), "e5m2": (ml_dtypes.float8_e5m2, 14)}[fmt]
    v = np.moveaxis(np.asarray(x, np.float32).astype(ml_dtypes.bfloat16).astype(np.float64), axis, -1)
    blocks = v.reshape(v.shape[:-1] + (-1, 32))
    amax = np.abs(blocks).max(-1, keepdims=True)
    byte = np.maximum(np.where(amax > 0, np.frexp(amax)[1] - 1 + 127, 0) - down, 1)
    scale = np.exp2(byte - 127.0)
    codes = (blocks / scale).astype(np.float32).astype(dtype).astype(np.float64)
    return np.moveaxis((codes * scale).reshape(v.shape), -1, axis)


WIDE = False


def mx_kscale(k):
    if not WIDE:
        return np.ones(k)
    levels = np.array([10, -10, 5, -5, 0])
    if k % 512:
        return np.exp2(np.random.permutation(np.resize(levels, k // 32))).repeat(32)
    a = np.empty((k // 512, 16))
    for p in range(k // 512):
        a[p, :8] = np.random.permutation(np.resize(levels, 8))
        for g in range(8):
            far = levels[np.abs(levels - a[p, g]) >= 10]
            a[p, g + 8] = far[np.random.randint(len(far))]
    return np.exp2(a.ravel()).repeat(32)


def f64(x):
    return np.asarray(x).astype(np.float64)


def striped(idx):
    return np.tile(idx.reshape(-1, 16).T, (8, 1)).astype(np.uint16)


def unstriped(offs):
    return offs[:16].T.reshape(-1).astype(np.int64)


E2M1 = np.array([0.0, 0.5, 1.0, 1.5, 2.0, 3.0, 4.0, 6.0, -0.0, -0.5, -1.0, -1.5, -2.0, -3.0, -4.0, -6.0])


def pack_weight(w, fmt):
    k, n = w.shape
    w = f64(np.asarray(w, np.float32).astype(ml_dtypes.bfloat16)).reshape(k // 32, 32, n)
    amax = np.abs(w).max(1)
    if fmt == "e4m3":
        byte = np.frexp(amax)[1] - 1 + 127 - 7
    else:
        mant, ex = np.frexp(amax / 6.0)
        byte = np.where(mant > 0.5, ex, ex - 1) + 127
    byte = np.clip(np.where(amax > 0, byte, 1), 1, 254)
    scaled = (w * np.exp2(127.0 - byte)[:, None, :]).reshape(k, n).astype(np.float32)
    by_word = np.ascontiguousarray(scaled.reshape(k // 512, 128, 4, n).transpose(0, 1, 3, 2))
    if fmt == "e4m3":
        words = by_word.astype(ml_dtypes.float8_e4m3fn).view(np.uint8)
    else:
        c = by_word.astype(ml_dtypes.float4_e2m1fn).view(np.uint8) & 0xF
        words = (c[..., 0::2] | (c[..., 1::2] << 4)).reshape(k // 512, 128, 2 * n)
    return np.ascontiguousarray(words), np.ascontiguousarray(byte.astype(np.uint8).reshape(k // 512, 16, n))


def unpack_weight(words, scales, fmt):
    g, _, n = scales.shape
    words = np.ascontiguousarray(words).reshape(g, 128, n, -1)
    if fmt == "e4m3":
        vals = words.view(ml_dtypes.float8_e4m3fn).astype(np.float64)
    else:
        nib = np.empty((g, 128, n, 4), np.uint8)
        nib[..., 0::2] = words & 0xF
        nib[..., 1::2] = words >> 4
        vals = E2M1[nib]
    vals = vals * np.repeat(np.exp2(scales.astype(np.float64) - 127.0), 8, axis=1)[..., None]
    return vals.transpose(0, 1, 3, 2).reshape(g * 512, n)


def gelu(v):
    return 0.5 * v * (1.0 + np.tanh(np.sqrt(2.0 / np.pi) * (v + 0.044715 * v**3)))


K, H, T, S, T3, S2, P = 512, 1024, 4096, 1024, 2048, 512, 512


def setup_inputs():
    n = np.random.standard_normal
    s = mx_kscale(K)[:, None]
    u = mx_kscale(H)[:, None]
    tab_words, tab_scales = pack_weight(n((K, T)) * s, "e4m3")
    tab2_words, tab2_scales = pack_weight(n((H, T3)) / np.sqrt(H) / u, "e4m3")
    w4_words, w4_scales = pack_weight(0.7 * n((K, H)) / np.sqrt(K) / s, "e2m1")
    return {
        "tab_words": tab_words,
        "tab_scales": tab_scales,
        "offs": striped(np.random.permutation(T)[:S]),
        "tab2_words": tab2_words,
        "tab2_scales": tab2_scales,
        "offs2": striped(np.random.permutation(T3)[:S2]),
        "pos1": striped(np.random.permutation(S)[:P]),
        "pos2": striped(np.random.permutation(S)[:P]),
        "w1": (1.5 * n((K, H)) / np.sqrt(K) / s).astype(np.float32),
        "w4_words": w4_words,
        "w4_scales": w4_scales,
        "gain": (np.exp(0.3 * n(H)) * u[:, 0]).astype(np.float32),
        "cabin": np.exp(0.5 * n((H, P))).astype(np.float32),
        "exc": n((S2, P)).astype(np.float32),
    }


def reference(tab_words, tab_scales, offs, tab2_words, tab2_scales, offs2, pos1, pos2,
              w1, w4_words, w4_scales, gain, cabin, exc):
    v = unpack_weight(tab_words, tab_scales, "e4m3")[:, unstriped(offs)]
    v2 = unpack_weight(tab2_words, tab2_scales, "e4m3")[:, unstriped(offs2)]
    w1q = mxq(f64(w1), 0, "e4m3")
    w4 = unpack_weight(w4_words, w4_scales, "e2m1")
    bent = np.tanh(w1q.T @ v)
    h = f64(gain)[:, None] * (bent + (w4.T @ v))
    x1 = mxq(h[:, unstriped(pos1)] * f64(cabin), 0, "e4m3")
    x2 = mxq(h[:, unstriped(pos2)], 0, "e4m3")
    e1 = v2.T @ x1
    e2 = v2.T @ x2
    return (e1 + f64(exc)) * e2

@@ -1,0 +1,238 @@
+from contextlib import ExitStack
+
+import concourse.mybir as mybir
+from concourse.masks import make_identity
+
+K, H, T, S, T3, S2, NP = 512, 1024, 4096, 1024, 2048, 512, 512
+FLOPS = 2 * (2 * K * H * S + 2 * H * S2 * NP)
+
+F32 = mybir.dt.float32
+BF16 = mybir.dt.bfloat16
+I32 = mybir.dt.int32
+U32 = mybir.dt.uint32
+U16 = mybir.dt.uint16
+U8 = mybir.dt.uint8
+FP8X4 = mybir.dt.float8_e4m3fn_x4
+FP4X4 = mybir.dt.float4_e2m1fn_x4
+ACT = mybir.ActivationFunctionType
+ALU = mybir.AluOpType
+
+P = 128
+PACK = 4
+KP = P * PACK
+NB = H // KP
+BANK = 512
+
+
+def weave_views(dst, src, c0, c1):
+    d = dst[:, c0:c1, :].rearrange("p (c i) t -> p c t i", i=4)
+    s = src[:, :, c0:c1].rearrange("p t (c i) -> p c t i", i=4)
+    return d, s
+
+
+def tile_list_excursion_pair_ranks_kernel(tc, tab_words, tab_scales, offs, tab2_words, tab2_scales, offs2,
+                                                    pos1, pos2, w1, w4_words, w4_scales, gain, cabin, exc, out):
+    nc = tc.nc
+    with ExitStack() as ctx:
+        lists = ctx.enter_context(tc.tile_pool(name="lists", bufs=1))
+        keep = ctx.enter_context(tc.tile_pool(name="keep", bufs=1))
+        ring = ctx.enter_context(tc.tile_pool(name="ring", bufs=1))
+        psum = ctx.enter_context(tc.psum_pool(name="psum", bufs=1))
+
+        idx = lists.tile([P, S // 16], U16, name="idx")
+        idx2 = lists.tile([P, S2 // 16], U16, name="idx2")
+        p1 = lists.tile([P, NP // 16], U16, name="p1")
+        p2 = lists.tile([P, NP // 16], U16, name="p2")
+
+        tab_w = keep.tile([P, T], I32, name="tab_w")
+        tab_s = keep.tile([P, T], U8, name="tab_s")
+        tab2_w = [keep.tile([P, T3], I32, name=f"tab2_w{a}") for a in range(NB)]
+        tab2_s = keep.tile([P, T3], U8, name="tab2_s")
+        w1_raw = [keep.tile([P, PACK, KP], F32, name=f"w1_raw{b}") for b in range(NB)]
+        w4_w = keep.tile([P, 2 * H], U8, name="w4_w", align_bytes=64)
+        w4_s = keep.tile([P, H], U8, name="w4_s", align_bytes=64)
+        gain_sb = [keep.tile([P, PACK], F32, name=f"gain{b}", tag=f"gain{b}", align_bytes=64) for b in range(NB)]
+        cabin_sb = [keep.tile([P, PACK, NP], F32, name=f"cabin{b}", tag=f"cabin{b}", align_bytes=64) for b in range(NB)]
+        exc_sb = keep.tile([P, S2 // P, NP], F32, name="exc_sb")
+        ident = keep.tile([P, P], F32, name="ident")
+
+        nc.vector.memset(tab_s[:].bitcast(I32), 0)
+        nc.gpsimd.memset(w4_s[:].bitcast(I32), 0)
+        nc.vector.memset(tab2_s[:].bitcast(I32), 0)
+
+        def load_w1(b):
+            nc.sync.dma_start(out=w1_raw[b][:], in_=w1[:, b * KP:(b + 1) * KP].rearrange("(p j) c -> p j c", j=PACK))
+
+        def load_cabin(b):
+            nc.sync.dma_start(out=cabin_sb[b][:], in_=cabin[b * KP:(b + 1) * KP, :].rearrange("(p t) n -> p t n", t=PACK))
+
+        nc.sync.dma_start(idx[:], offs)
+        load_w1(0)
+        for q in range(4):
+            nc.sync.dma_start(out=tab_s[32 * q:32 * q + 4, :].bitcast(I32), in_=tab_scales[0, 4 * q:4 * q + 4, :].bitcast(I32))
+        nc.sync.dma_start(out=tab_w[:], in_=tab_words[0].rearrange("p t i -> p (t i)").bitcast(I32))
+        nc.sync.dma_start(out=w4_w[:].bitcast(I32), in_=w4_words[0].bitcast(I32))
+        for q in range(4):
+            nc.sync.dma_start(out=w4_s[32 * q:32 * q + 4, :].bitcast(I32), in_=w4_scales[0, 4 * q:4 * q + 4, :].bitcast(I32))
+        make_identity(nc, ident[:])
+        load_w1(1)
+        for b in range(NB):
+            nc.sync.dma_start(out=gain_sb[b][:], in_=gain[b * KP:(b + 1) * KP].rearrange("(p t) -> p t", t=PACK))
+        nc.sync.dma_start(p1[:], pos1)
+        nc.sync.dma_start(p2[:], pos2)
+        load_cabin(0)
+        nc.sync.dma_start(idx2[:], offs2)
+        for q in range(4):
+            nc.sync.dma_start(out=tab2_s[32 * q:32 * q + 4 * NB, :].bitcast(I32), in_=tab2_scales[:, 4 * q:4 * q + 4, :].bitcast(I32))
+        for a in range(NB):
+            nc.sync.dma_start(out=tab2_w[a][:], in_=tab2_words[a].rearrange("p t i -> p (t i)").bitcast(I32))
+        load_cabin(1)
+        nc.sync.dma_start(out=exc_sb[:], in_=exc.rearrange("(a p) n -> p a n", p=P))
+
+        def woven_tile(name):
+            return ring.tile([P, KP, PACK], BF16, name=name, tag="woven", bufs=3, align_bytes=64)
+
+        def quantise(woven, name):
+            codes = keep.tile([P, KP], U32, name=name + "_codes", align_bytes=64)
+            scales = keep.tile([P, KP], U8, name=name + "_scales", align_bytes=64)
+            nc.vector.quantize_mx(out=codes[:].bitcast(FP8X4), scales=scales[:], in_=woven[:].rearrange("p n t -> p (n t)"))
+            return codes, scales
+
+        w1_woven = [woven_tile(f"w1_woven{b}") for b in range(NB)]
+        d, s = weave_views(w1_woven[0], w1_raw[0], 0, KP)
+        nc.scalar.copy(out=d, in_=s)
+        v_s = keep.tile([P, S], U8, name="v_s", align_bytes=64)
+        nc.vector.tensor_copy(out=v_s[:], in_=tab_s[:].indirect(idx[:]))
+        w1_q = [quantise(w1_woven[0], "w1q0")]
+        VG = 256
+        v_w = []
+        for g in range(S // VG):
+            piece = keep.tile([P, VG], U32, name=f"v_w{g}", align_bytes=64)
+            nc.vector.tensor_copy(out=piece[:], in_=tab_w[:].bitcast(U32).indirect(idx[:, g * VG // 16:(g + 1) * VG // 16]))
+            v_w.append(piece)
+        d, s = weave_views(w1_woven[1], w1_raw[1], 0, KP)
+        nc.gpsimd.tensor_scalar(out=d, in0=s, scalar1=1.0, scalar2=0.0, op0=ALU.mult, op1=ALU.add)
+
+        def by_slot(bank):
+            return bank[:].rearrange("j (q t) -> j t q", t=PACK)
+
+        def bank_tile(k, name):
+            return psum.tile([P, BANK], F32, name=name, tag=f"bank{k}")
+
+        def unit(b, jc, add_on_vector, banks):
+            words = v_w[jc * P // VG][:, jc * P % VG:jc * P % VG + P].bitcast(FP8X4)
+            scale = v_s[:, jc * P:(jc + 1) * P]
+            a_bank = bank_tile((2 * jc) % banks, "a_bank")
+            nc.tensor.matmul_mx(out=a_bank[:], lhsT=words, lhsT_scale=scale, rhs=w1_q[b][0][:].bitcast(FP8X4),
+                                rhs_scale=w1_q[b][1][:], start=True, stop=True)
+            b_bank = bank_tile((2 * jc + 1) % banks, "b_bank")
+            nc.tensor.matmul_mx(out=b_bank[:], lhsT=words, lhsT_scale=scale,
+                                rhs=w4_w[:, 2 * b * KP:2 * (b + 1) * KP].bitcast(FP4X4),
+                                rhs_scale=w4_s[:, b * KP:(b + 1) * KP], start=True, stop=True)
+            if jc == 7 and b == 0:
+                bent = keep.tile([P, PACK, P], F32, name="bent", tag="last0", align_bytes=64)
+            else:
+                bent = ring.tile([P, PACK, P], F32, name="bent", tag="bent", bufs=8)
+            nc.scalar.activation(out=bent[:], in_=by_slot(a_bank), func=ACT.Tanh)
+            other = ring.tile([P, PACK, P], F32, name="other", tag="other", bufs=10)
+            if add_on_vector:
+                nc.vector.tensor_tensor(out=other[:], in0=by_slot(b_bank), in1=bent[:], op=ALU.add)
+                return [other]
+            nc.scalar.copy(out=other[:], in_=by_slot(b_bank))
+            return [other, bent]
+
+        def turn(parts, t, half, k):
+            bank = bank_tile(k, "h_bank")
+            for c in range(4):
+                terms = parts[4 * half + c]
+                for i, term in enumerate(terms):
+                    nc.tensor.matmul(out=bank[:, c * P:(c + 1) * P], lhsT=term[:, t, :], rhs=ident[:], is_transpose=True,
+                                     start=(i == 0), stop=(i == len(terms) - 1))
+            return bank
+
+        def land(h, bank, b, t, half):
+            nc.scalar.activation(out=h[:, half * BANK:(half + 1) * BANK], in_=bank[:], func=ACT.Copy,
+                                 scale=gain_sb[b][:, t:t + 1])
+
+        x1_rows = [keep.tile([P, PACK, NP], F32, name=f"x1_rows{b}") for b in range(NB)]
+        x2_rows = [keep.tile([P, PACK, NP], BF16, name="x2_rows0")]
+
+        def pick1(h, b, t):
+            nc.vector.tensor_tensor(out=x1_rows[b][:, t, :], in0=h[:].indirect(p1[:]), in1=cabin_sb[b][:, t, :], op=ALU.mult)
+
+        def pick2(h, b, t):
+            nc.vector.tensor_copy(out=x2_rows[b][:, t, :], in_=h[:].indirect(p2[:]))
+
+        hs = [[keep.tile([P, S], F32, name=f"h{b}{t}") for t in range(PACK)] for b in range(NB)]
+
+        def rows_of(b, t, parts, first_bank):
+            for half in range(2):
+                land(hs[b][t], turn(parts, t, half, (first_bank + 2 * t + half) % 8), b, t, half)
+
+        parts0 = [unit(0, jc, True, 8) for jc in range(8)]
+        w1_q.append(quantise(w1_woven[1], "w1q1"))
+        v2_s = keep.tile([P, S2], U8, name="v2_s", tag="last0", align_bytes=64)
+        nc.vector.tensor_copy(out=v2_s[:], in_=tab2_s[:].indirect(idx2[:]))
+        parts1 = []
+        for t in range(PACK):
+            rows_of(0, t, parts0, 0)
+            pick2(hs[0][t], 0, t)
+            pick1(hs[0][t], 0, t)
+            if t >= 1:
+                parts1.append(unit(1, t - 1, False, 4))
+        v2_w = keep.tile([P, NB, S2], U32, name="v2_w", tag="cabin0", align_bytes=64)
+        for a in range(NB):
+            nc.vector.tensor_copy(out=v2_w[:, a, :], in_=tab2_w[a][:].bitcast(U32).indirect(idx2[:]))
+        x2_woven = [woven_tile("x2_woven0")]
+        d, s = weave_views(x2_woven[0], x2_rows[0], 0, NP)
+        nc.vector.tensor_copy(out=d, in_=s)
+        for jc in range(PACK - 1, 8):
+            parts1.append(unit(1, jc, False, 4))
+        for t in range(PACK):
+            rows_of(1, t, parts1, 4)
+            pick1(hs[1][t], 1, t)
+        x2_q = [quantise(x2_woven[0], "x2q0")]
+
+        def weave_on_scalar(woven, rows, n0):
+            for c0 in range(0, rows.shape[2], P):
+                dd = woven[:, n0 + c0:n0 + c0 + P, :].rearrange("p (c i) t -> p c t i", i=4)
+                ss = rows[:, :, c0:c0 + P].rearrange("p t (c i) -> p c t i", i=4)
+                nc.scalar.copy(out=dd, in_=ss)
+            return woven
+
+        x1_woven = [weave_on_scalar(keep.tile([P, KP, PACK], BF16, name="x1_woven0", tag="gain1", align_bytes=64), x1_rows[0], 0),
+                    weave_on_scalar(keep.tile([P, KP, PACK], BF16, name="x1_woven1", tag="late", align_bytes=64), x1_rows[1], 0)]
+        HN = NP // 2
+        x2_woven.append(woven_tile("x2_woven1"))
+
+        def late_picks(half, tag):
+            rows = keep.tile([P, PACK, HN], BF16, name=f"x2_late{half}", tag=tag, align_bytes=64)
+            for t in range(PACK):
+                nc.vector.tensor_copy(out=rows[:, t, :], in_=hs[1][t][:].indirect(p2[:, half * HN // 16:(half + 1) * HN // 16]))
+            weave_on_scalar(x2_woven[1], rows, half * HN)
+
+        late_picks(0, "cabin1")
+        x1_q = [quantise(x1_woven[b], f"x1q{b}") for b in range(NB)]
+        late_picks(1, "late")
+
+        def score_pass(bank, m, a, xq):
+            nc.tensor.matmul_mx(out=bank[:], lhsT=v2_w[:, a, m * P:(m + 1) * P].bitcast(FP8X4),
+                                lhsT_scale=v2_s[4 * a:P, m * P:(m + 1) * P], rhs=xq[0][:].bitcast(FP8X4), rhs_scale=xq[1][:],
+                                start=(a == 0), stop=(a == NB - 1))
+
+        MT = S2 // P
+        e1 = [bank_tile(4 + m, f"e1_{m}") for m in range(MT)]
+        e2 = [bank_tile(m, f"e2_{m}") for m in range(MT)]
+        for m in range(MT):
+            for a in range(NB):
+                score_pass(e1[m], m, a, x1_q[a])
+        for m in range(MT):
+            score_pass(e2[m], m, 0, x2_q[0])
+        shifted = [keep.tile([P, NP], F32, name=f"shifted{m}") for m in range(MT)]
+        x2_q.append(quantise(x2_woven[1], "x2q1"))
+        for m in range(MT):
+            nc.vector.tensor_tensor(out=shifted[m][:], in0=e1[m][:], in1=exc_sb[:, m, :], op=ALU.add)
+        for m in range(MT):
+            score_pass(e2[m], m, 1, x2_q[1])
+            nc.vector.tensor_tensor(out=shifted[m][:], in0=e2[m][:], in1=shifted[m][:], op=ALU.mult)
+            nc.sync.dma_start(out=out[m * P:(m + 1) * P, :], in_=shifted[m][:])

@@ -22,6 +22,7 @@ PACK = 4
 KP = P * PACK
 NB = H // KP
 BANK = 512
+GADD = 4
 
 
 def weave_views(dst, src, c0, c1):
@@ -37,6 +38,7 @@ def tile_list_excursion_pair_ranks_kernel(tc, tab_words, tab_scales, offs, tab2_
         lists = ctx.enter_context(tc.tile_pool(name="lists", bufs=1))
         keep = ctx.enter_context(tc.tile_pool(name="keep", bufs=1))
         ring = ctx.enter_context(tc.tile_pool(name="ring", bufs=1))
+        shared = ctx.enter_context(tc.tile_pool(name="shared", bufs=1))
         psum = ctx.enter_context(tc.psum_pool(name="psum", bufs=1))
 
         idx = lists.tile([P, S // 16], U16, name="idx")
@@ -90,15 +92,15 @@ def tile_list_excursion_pair_ranks_kernel(tc, tab_words, tab_scales, offs, tab2_
         nc.sync.dma_start(out=exc_sb[:], in_=exc.rearrange("(a p) n -> p a n", p=P))
 
         def woven_tile(name):
-            return ring.tile([P, KP, PACK], BF16, name=name, tag="woven", bufs=3, align_bytes=64)
+            return ring.tile([P, KP, PACK], BF16, name=name, tag="woven", bufs=2, align_bytes=64)
 
-        def quantise(woven, name):
-            codes = keep.tile([P, KP], U32, name=name + "_codes", align_bytes=64)
+        def quantise(woven, name, tag=None):
+            codes = keep.tile([P, KP], U32, name=name + "_codes", tag=tag or name, align_bytes=64)
             scales = keep.tile([P, KP], U8, name=name + "_scales", align_bytes=64)
             nc.vector.quantize_mx(out=codes[:].bitcast(FP8X4), scales=scales[:], in_=woven[:].rearrange("p n t -> p (n t)"))
             return codes, scales
 
-        w1_woven = [woven_tile(f"w1_woven{b}") for b in range(NB)]
+        w1_woven = [woven_tile("w1_woven0"), keep.tile([P, KP, PACK], BF16, name="w1_woven1", tag="w1_woven1", align_bytes=64)]
         d, s = weave_views(w1_woven[0], w1_raw[0], 0, KP)
         nc.scalar.copy(out=d, in_=s)
         v_s = keep.tile([P, S], U8, name="v_s", align_bytes=64)
@@ -110,8 +112,7 @@ def tile_list_excursion_pair_ranks_kernel(tc, tab_words, tab_scales, offs, tab2_
             piece = keep.tile([P, VG], U32, name=f"v_w{g}", align_bytes=64)
             nc.vector.tensor_copy(out=piece[:], in_=tab_w[:].bitcast(U32).indirect(idx[:, g * VG // 16:(g + 1) * VG // 16]))
             v_w.append(piece)
-        d, s = weave_views(w1_woven[1], w1_raw[1], 0, KP)
-        nc.gpsimd.tensor_scalar(out=d, in0=s, scalar1=1.0, scalar2=0.0, op0=ALU.mult, op1=ALU.add)
+        nc.gpsimd.tensor_scalar(out=w1_woven[1][:], in0=w1_raw[1][:].rearrange("p j c -> p c j"), scalar1=1.0, scalar2=0.0, op0=ALU.mult, op1=ALU.add)
 
         def by_slot(bank):
             return bank[:].rearrange("j (q t) -> j t q", t=PACK)
@@ -130,7 +131,9 @@ def tile_list_excursion_pair_ranks_kernel(tc, tab_words, tab_scales, offs, tab2_
                                 rhs=w4_w[:, 2 * b * KP:2 * (b + 1) * KP].bitcast(FP4X4),
                                 rhs_scale=w4_s[:, b * KP:(b + 1) * KP], start=True, stop=True)
             if jc == 7 and b == 0:
-                bent = keep.tile([P, PACK, P], F32, name="bent", tag="last0", align_bytes=64)
+                bent = shared.tile([P, PACK, P], F32, name="bent_last", offset=0, align_bytes=64)
+            elif jc == 7:
+                bent = keep.tile([P, PACK, P], F32, name="bent", tag=f"last{b}", align_bytes=64)
             else:
                 bent = ring.tile([P, PACK, P], F32, name="bent", tag="bent", bufs=8)
             nc.scalar.activation(out=bent[:], in_=by_slot(a_bank), func=ACT.Tanh)
@@ -155,43 +158,42 @@ def tile_list_excursion_pair_ranks_kernel(tc, tab_words, tab_scales, offs, tab2_
                                  scale=gain_sb[b][:, t:t + 1])
 
         x1_rows = [keep.tile([P, PACK, NP], F32, name=f"x1_rows{b}") for b in range(NB)]
-        x2_rows = [keep.tile([P, PACK, NP], BF16, name="x2_rows0")]
 
         def pick1(h, b, t):
             nc.vector.tensor_tensor(out=x1_rows[b][:, t, :], in0=h[:].indirect(p1[:]), in1=cabin_sb[b][:, t, :], op=ALU.mult)
 
-        def pick2(h, b, t):
-            nc.vector.tensor_copy(out=x2_rows[b][:, t, :], in_=h[:].indirect(p2[:]))
+        def weave_on_gpsimd(woven, rows):
+            nc.gpsimd.tensor_scalar(out=woven[:], in0=rows[:].rearrange("p t n -> p n t"), scalar1=1.0, scalar2=0.0, op0=ALU.mult, op1=ALU.add)
+            return woven
 
         hs = [[keep.tile([P, S], F32, name=f"h{b}{t}") for t in range(PACK)] for b in range(NB)]
 
         def rows_of(b, t, parts, first_bank):
             for half in range(2):
-                land(hs[b][t], turn(parts, t, half, (first_bank + 2 * t + half) % 8), b, t, half)
+                land(hs[b][t], turn(parts, t, half, first_bank + half), b, t, half)
 
-        parts0 = [unit(0, jc, True, 8) for jc in range(8)]
+        parts0 = [unit(0, jc, True, 8) for jc in range(6)]
         w1_q.append(quantise(w1_woven[1], "w1q1"))
-        v2_s = keep.tile([P, S2], U8, name="v2_s", tag="last0", align_bytes=64)
+        parts0 = parts0 + [unit(0, jc, True, 8) for jc in range(6, 8)]
+        v2_s = shared.tile([P, S2], U8, name="v2_s", offset=0, align_bytes=64)
         nc.vector.tensor_copy(out=v2_s[:], in_=tab2_s[:].indirect(idx2[:]))
-        parts1 = []
-        for t in range(PACK):
-            rows_of(0, t, parts0, 0)
-            pick2(hs[0][t], 0, t)
-            pick1(hs[0][t], 0, t)
-            if t >= 1:
-                parts1.append(unit(1, t - 1, False, 4))
-        v2_w = keep.tile([P, NB, S2], U32, name="v2_w", tag="cabin0", align_bytes=64)
+        v2_w = shared.tile([P, NB, S2], U32, name="v2_w", offset=S2, align_bytes=64)
         for a in range(NB):
             nc.vector.tensor_copy(out=v2_w[:, a, :], in_=tab2_w[a][:].bitcast(U32).indirect(idx2[:]))
-        x2_woven = [woven_tile("x2_woven0")]
-        d, s = weave_views(x2_woven[0], x2_rows[0], 0, NP)
-        nc.vector.tensor_copy(out=d, in_=s)
-        for jc in range(PACK - 1, 8):
+        parts1 = []
+        for t in range(PACK):
+            rows_of(0, t, parts0, 4 + 2 * (t % 2))
+            pick1(hs[0][t], 0, t)
+            parts1.append(unit(1, t, False, 4))
+        x1_woven = [weave_on_gpsimd(keep.tile([P, KP, PACK], BF16, name="x1_woven0", align_bytes=64), x1_rows[0])]
+        x2_rows = keep.tile([P, PACK, NP], BF16, name="x2_rows0", tag="cabin0", align_bytes=64)
+        for t in range(PACK):
+            nc.vector.tensor_copy(out=x2_rows[:, t, :], in_=hs[0][t][:].indirect(p2[:]))
+        for jc in range(PACK, 8):
             parts1.append(unit(1, jc, False, 4))
         for t in range(PACK):
-            rows_of(1, t, parts1, 4)
+            rows_of(1, t, parts1, (4 + 2 * t) % 8)
             pick1(hs[1][t], 1, t)
-        x2_q = [quantise(x2_woven[0], "x2q0")]
 
         def weave_on_scalar(woven, rows, n0):
             for c0 in range(0, rows.shape[2], P):
@@ -200,10 +202,10 @@ def tile_list_excursion_pair_ranks_kernel(tc, tab_words, tab_scales, offs, tab2_
                 nc.scalar.copy(out=dd, in_=ss)
             return woven
 
-        x1_woven = [weave_on_scalar(keep.tile([P, KP, PACK], BF16, name="x1_woven0", tag="gain1", align_bytes=64), x1_rows[0], 0),
-                    weave_on_scalar(keep.tile([P, KP, PACK], BF16, name="x1_woven1", tag="late", align_bytes=64), x1_rows[1], 0)]
+        x1_woven.append(weave_on_scalar(keep.tile([P, KP, PACK], BF16, name="x1_woven1", tag="late", align_bytes=64), x1_rows[1], 0))
         HN = NP // 2
-        x2_woven.append(woven_tile("x2_woven1"))
+        x2_woven = [weave_on_gpsimd(keep.tile([P, KP, PACK], BF16, name="x2_woven0", tag="cabin1", align_bytes=64), x2_rows),
+                    woven_tile("x2_woven1")]
 
         def late_picks(half, tag):
             rows = keep.tile([P, PACK, HN], BF16, name=f"x2_late{half}", tag=tag, align_bytes=64)
@@ -211,9 +213,11 @@ def tile_list_excursion_pair_ranks_kernel(tc, tab_words, tab_scales, offs, tab2_
                 nc.vector.tensor_copy(out=rows[:, t, :], in_=hs[1][t][:].indirect(p2[:, half * HN // 16:(half + 1) * HN // 16]))
             weave_on_scalar(x2_woven[1], rows, half * HN)
 
-        late_picks(0, "cabin1")
-        x1_q = [quantise(x1_woven[b], f"x1q{b}") for b in range(NB)]
+        x1_q = [quantise(x1_woven[0], "x1q0", "last1")]
+        late_picks(0, "gain1")
+        x1_q.append(quantise(x1_woven[1], "x1q1"))
         late_picks(1, "late")
+        x2_q = [quantise(x2_woven[0], "x2q0")]
 
         def score_pass(bank, m, a, xq):
             nc.tensor.matmul_mx(out=bank[:], lhsT=v2_w[:, a, m * P:(m + 1) * P].bitcast(FP8X4),
@@ -223,16 +227,21 @@ def tile_list_excursion_pair_ranks_kernel(tc, tab_words, tab_scales, offs, tab2_
         MT = S2 // P
         e1 = [bank_tile(4 + m, f"e1_{m}") for m in range(MT)]
         e2 = [bank_tile(m, f"e2_{m}") for m in range(MT)]
-        for m in range(MT):
-            for a in range(NB):
+        for a in range(NB):
+            for m in reversed(range(MT)):
                 score_pass(e1[m], m, a, x1_q[a])
         for m in range(MT):
             score_pass(e2[m], m, 0, x2_q[0])
         shifted = [keep.tile([P, NP], F32, name=f"shifted{m}") for m in range(MT)]
         x2_q.append(quantise(x2_woven[1], "x2q1"))
-        for m in range(MT):
+        for m in reversed(range(MT)):
+            if m >= GADD:
+                nc.scalar.copy(out=shifted[m][:], in_=e1[m][:])
+                nc.gpsimd.tensor_tensor(out=shifted[m][:], in0=shifted[m][:], in1=exc_sb[:, m, :], op=ALU.add)
+        for m in range(GADD):
             nc.vector.tensor_tensor(out=shifted[m][:], in0=e1[m][:], in1=exc_sb[:, m, :], op=ALU.add)
         for m in range(MT):
             score_pass(e2[m], m, 1, x2_q[1])
+        for m in range(MT):
             nc.vector.tensor_tensor(out=shifted[m][:], in0=e2[m][:], in1=shifted[m][:], op=ALU.mult)
             nc.sync.dma_start(out=out[m * P:(m + 1) * P, :], in_=shifted[m][:])

@@ -22,7 +22,6 @@ PACK = 4
 KP = P * PACK
 NB = H // KP
 BANK = 512
-GADD = 4
 
 
 def weave_views(dst, src, c0, c1):
@@ -39,6 +38,7 @@ def tile_list_excursion_pair_ranks_kernel(tc, tab_words, tab_scales, offs, tab2_
         keep = ctx.enter_context(tc.tile_pool(name="keep", bufs=1))
         ring = ctx.enter_context(tc.tile_pool(name="ring", bufs=1))
         shared = ctx.enter_context(tc.tile_pool(name="shared", bufs=1))
+        tail = ctx.enter_context(tc.tile_pool(name="tail", bufs=1))
         psum = ctx.enter_context(tc.psum_pool(name="psum", bufs=1))
 
         idx = lists.tile([P, S // 16], U16, name="idx")
@@ -46,7 +46,7 @@ def tile_list_excursion_pair_ranks_kernel(tc, tab_words, tab_scales, offs, tab2_
         p1 = lists.tile([P, NP // 16], U16, name="p1")
         p2 = lists.tile([P, NP // 16], U16, name="p2")
 
-        tab_w = keep.tile([P, T], I32, name="tab_w")
+        tab_w = keep.tile([P, T], I32, name="tab_w", tag="tab_w", align_bytes=64)
         tab_s = keep.tile([P, T], U8, name="tab_s")
         tab2_w = [keep.tile([P, T3], I32, name=f"tab2_w{a}") for a in range(NB)]
         tab2_s = keep.tile([P, T3], U8, name="tab2_s")
@@ -92,7 +92,7 @@ def tile_list_excursion_pair_ranks_kernel(tc, tab_words, tab_scales, offs, tab2_
         nc.sync.dma_start(out=exc_sb[:], in_=exc.rearrange("(a p) n -> p a n", p=P))
 
         def woven_tile(name):
-            return ring.tile([P, KP, PACK], BF16, name=name, tag="woven", bufs=2, align_bytes=64)
+            return ring.tile([P, KP, PACK], BF16, name=name, tag="woven", bufs=1, align_bytes=64)
 
         def quantise(woven, name, tag=None):
             codes = keep.tile([P, KP], U32, name=name + "_codes", tag=tag or name, align_bytes=64)
@@ -100,7 +100,7 @@ def tile_list_excursion_pair_ranks_kernel(tc, tab_words, tab_scales, offs, tab2_
             nc.vector.quantize_mx(out=codes[:].bitcast(FP8X4), scales=scales[:], in_=woven[:].rearrange("p n t -> p (n t)"))
             return codes, scales
 
-        w1_woven = [woven_tile("w1_woven0"), keep.tile([P, KP, PACK], BF16, name="w1_woven1", tag="w1_woven1", align_bytes=64)]
+        w1_woven = [woven_tile("w1_woven0")]
         d, s = weave_views(w1_woven[0], w1_raw[0], 0, KP)
         nc.scalar.copy(out=d, in_=s)
         v_s = keep.tile([P, S], U8, name="v_s", align_bytes=64)
@@ -109,9 +109,10 @@ def tile_list_excursion_pair_ranks_kernel(tc, tab_words, tab_scales, offs, tab2_
         VG = 256
         v_w = []
         for g in range(S // VG):
-            piece = keep.tile([P, VG], U32, name=f"v_w{g}", align_bytes=64)
+            piece = keep.tile([P, VG], U32, name=f"v_w{g}", tag=f"v_w{g}", align_bytes=64)
             nc.vector.tensor_copy(out=piece[:], in_=tab_w[:].bitcast(U32).indirect(idx[:, g * VG // 16:(g + 1) * VG // 16]))
             v_w.append(piece)
+        w1_woven.append(keep.tile([P, KP, PACK], BF16, name="w1_woven1", tag="tab_w", align_bytes=64))
         nc.gpsimd.tensor_scalar(out=w1_woven[1][:], in0=w1_raw[1][:].rearrange("p j c -> p c j"), scalar1=1.0, scalar2=0.0, op0=ALU.mult, op1=ALU.add)
 
         def by_slot(bank):
@@ -181,42 +182,46 @@ def tile_list_excursion_pair_ranks_kernel(tc, tab_words, tab_scales, offs, tab2_
         for a in range(NB):
             nc.vector.tensor_copy(out=v2_w[:, a, :], in_=tab2_w[a][:].bitcast(U32).indirect(idx2[:]))
         parts1 = []
+        x2_rows = keep.tile([P, PACK, NP], BF16, name="x2_rows0")
         for t in range(PACK):
             rows_of(0, t, parts0, 4 + 2 * (t % 2))
             pick1(hs[0][t], 0, t)
-            parts1.append(unit(1, t, False, 4))
-        x1_woven = [weave_on_gpsimd(keep.tile([P, KP, PACK], BF16, name="x1_woven0", align_bytes=64), x1_rows[0])]
-        x2_rows = keep.tile([P, PACK, NP], BF16, name="x2_rows0", tag="cabin0", align_bytes=64)
-        for t in range(PACK):
             nc.vector.tensor_copy(out=x2_rows[:, t, :], in_=hs[0][t][:].indirect(p2[:]))
+            parts1.append(unit(1, t, False, 4))
+        x1_woven = [keep.tile([P, KP, PACK], BF16, name="x1_woven0", tag="v_w3", align_bytes=64)]
+        d, s = weave_views(x1_woven[0], x1_rows[0], 0, 256)
+        nc.vector.tensor_copy(out=d, in_=s)
         for jc in range(PACK, 8):
             parts1.append(unit(1, jc, False, 4))
         for t in range(PACK):
             rows_of(1, t, parts1, (4 + 2 * t) % 8)
             pick1(hs[1][t], 1, t)
 
-        def weave_on_scalar(woven, rows, n0):
-            for c0 in range(0, rows.shape[2], P):
+        def weave_on_scalar(woven, rows, n0, first=0):
+            for c0 in range(first, rows.shape[2], P):
                 dd = woven[:, n0 + c0:n0 + c0 + P, :].rearrange("p (c i) t -> p c t i", i=4)
                 ss = rows[:, :, c0:c0 + P].rearrange("p t (c i) -> p c t i", i=4)
                 nc.scalar.copy(out=dd, in_=ss)
             return woven
 
+        weave_on_scalar(x1_woven[0], x1_rows[0], 0, 256)
         x1_woven.append(weave_on_scalar(keep.tile([P, KP, PACK], BF16, name="x1_woven1", tag="late", align_bytes=64), x1_rows[1], 0))
-        HN = NP // 2
-        x2_woven = [weave_on_gpsimd(keep.tile([P, KP, PACK], BF16, name="x2_woven0", tag="cabin1", align_bytes=64), x2_rows),
-                    woven_tile("x2_woven1")]
+        HN = 384
+        x2_woven = [keep.tile([P, KP, PACK], BF16, name="x2_woven0", tag="last1", align_bytes=64),
+                    tail.tile([P, KP, PACK], BF16, name="x2_woven1", offset=0, align_bytes=64)]
 
-        def late_picks(half, tag):
-            rows = keep.tile([P, PACK, HN], BF16, name=f"x2_late{half}", tag=tag, align_bytes=64)
+        def late_picks(n0, n1, tag):
+            rows = keep.tile([P, PACK, n1 - n0], BF16, name=f"x2_late{n0}", tag=tag, align_bytes=64)
             for t in range(PACK):
-                nc.vector.tensor_copy(out=rows[:, t, :], in_=hs[1][t][:].indirect(p2[:, half * HN // 16:(half + 1) * HN // 16]))
-            weave_on_scalar(x2_woven[1], rows, half * HN)
+                nc.vector.tensor_copy(out=rows[:, t, :], in_=hs[1][t][:].indirect(p2[:, n0 // 16:n1 // 16]))
+            weave_on_scalar(x2_woven[1], rows, n0)
 
-        x1_q = [quantise(x1_woven[0], "x1q0", "last1")]
-        late_picks(0, "gain1")
+        weave_on_scalar(x2_woven[0], x2_rows, 0)
+        x1_q = [quantise(x1_woven[0], "x1q0")]
+        late_picks(0, P, "x2_late0")
+        late_picks(P, HN, "gain1")
         x1_q.append(quantise(x1_woven[1], "x1q1"))
-        late_picks(1, "late")
+        late_picks(HN, NP, "late")
         x2_q = [quantise(x2_woven[0], "x2q0")]
 
         def score_pass(bank, m, a, xq):
@@ -228,18 +233,22 @@ def tile_list_excursion_pair_ranks_kernel(tc, tab_words, tab_scales, offs, tab2_
         e1 = [bank_tile(4 + m, f"e1_{m}") for m in range(MT)]
         e2 = [bank_tile(m, f"e2_{m}") for m in range(MT)]
         for a in range(NB):
-            for m in reversed(range(MT)):
+            for m in range(MT):
                 score_pass(e1[m], m, a, x1_q[a])
         for m in range(MT):
             score_pass(e2[m], m, 0, x2_q[0])
-        shifted = [keep.tile([P, NP], F32, name=f"shifted{m}") for m in range(MT)]
+        def shift(m, tile):
+            nc.vector.tensor_tensor(out=tile[:], in0=e1[m][:], in1=exc_sb[:, m, :], op=ALU.add)
+            return tile
+
+        shifted = [shift(0, keep.tile([P, NP], F32, name="shifted0")),
+                   shift(1, keep.tile([P, NP], F32, name="shifted1", tag="last1", align_bytes=64))]
         x2_q.append(quantise(x2_woven[1], "x2q1"))
-        for m in reversed(range(MT)):
-            if m >= GADD:
-                nc.scalar.copy(out=shifted[m][:], in_=e1[m][:])
-                nc.gpsimd.tensor_tensor(out=shifted[m][:], in0=shifted[m][:], in1=exc_sb[:, m, :], op=ALU.add)
-        for m in range(GADD):
-            nc.vector.tensor_tensor(out=shifted[m][:], in0=e1[m][:], in1=exc_sb[:, m, :], op=ALU.add)
+        e1_last = keep.tile([P, NP], F32, name="e1_last")
+        nc.scalar.copy(out=e1_last[:], in_=e1[3][:])
+        shifted.append(shift(2, tail.tile([P, NP], F32, name="shifted2", offset=0, align_bytes=64)))
+        shifted.append(tail.tile([P, NP], F32, name="shifted3", offset=4 * NP, align_bytes=64))
+        nc.gpsimd.tensor_tensor(out=shifted[3][:], in0=e1_last[:], in1=exc_sb[:, 3, :], op=ALU.add)
         for m in range(MT):
             score_pass(e2[m], m, 1, x2_q[1])
         for m in range(MT):

@@ -47,7 +47,7 @@ def tile_list_excursion_pair_ranks_kernel(tc, tab_words, tab_scales, offs, tab2_
         p2 = lists.tile([P, NP // 16], U16, name="p2")
 
         tab_w = keep.tile([P, T], I32, name="tab_w", tag="tab_w", align_bytes=64)
-        tab_s = keep.tile([P, T], U8, name="tab_s")
+        tab_s = keep.tile([P, T], U8, name="tab_s", tag="tab_s", align_bytes=64)
         tab2_w = [keep.tile([P, T3], I32, name=f"tab2_w{a}") for a in range(NB)]
         tab2_s = keep.tile([P, T3], U8, name="tab2_s")
         w1_raw = [keep.tile([P, PACK, KP], F32, name=f"w1_raw{b}") for b in range(NB)]
@@ -68,26 +68,32 @@ def tile_list_excursion_pair_ranks_kernel(tc, tab_words, tab_scales, offs, tab2_
         def load_cabin(b):
             nc.sync.dma_start(out=cabin_sb[b][:], in_=cabin[b * KP:(b + 1) * KP, :].rearrange("(p t) n -> p t n", t=PACK))
 
+        def load_gain(b):
+            nc.sync.dma_start(out=gain_sb[b][:], in_=gain[b * KP:(b + 1) * KP].rearrange("(p t) -> p t", t=PACK))
+
+        def load_tab2(a):
+            nc.sync.dma_start(out=tab2_w[a][:], in_=tab2_words[a].rearrange("p t i -> p (t i)").bitcast(I32))
+
         nc.sync.dma_start(idx[:], offs)
         load_w1(0)
         for q in range(4):
-            nc.sync.dma_start(out=tab_s[32 * q:32 * q + 4, :].bitcast(I32), in_=tab_scales[0, 4 * q:4 * q + 4, :].bitcast(I32))
+            nc.sync.dma_start(out=tab_s[q:P:32, :].bitcast(I32), in_=tab_scales[0, q:16:4, :].bitcast(I32))
         nc.sync.dma_start(out=tab_w[:], in_=tab_words[0].rearrange("p t i -> p (t i)").bitcast(I32))
         nc.sync.dma_start(out=w4_w[:].bitcast(I32), in_=w4_words[0].bitcast(I32))
         for q in range(4):
-            nc.sync.dma_start(out=w4_s[32 * q:32 * q + 4, :].bitcast(I32), in_=w4_scales[0, 4 * q:4 * q + 4, :].bitcast(I32))
+            nc.sync.dma_start(out=w4_s[q:P:32, :].bitcast(I32), in_=w4_scales[0, q:16:4, :].bitcast(I32))
         make_identity(nc, ident[:])
         load_w1(1)
-        for b in range(NB):
-            nc.sync.dma_start(out=gain_sb[b][:], in_=gain[b * KP:(b + 1) * KP].rearrange("(p t) -> p t", t=PACK))
-        nc.sync.dma_start(p1[:], pos1)
-        nc.sync.dma_start(p2[:], pos2)
-        load_cabin(0)
+        load_gain(0)
         nc.sync.dma_start(idx2[:], offs2)
         for q in range(4):
             nc.sync.dma_start(out=tab2_s[32 * q:32 * q + 4 * NB, :].bitcast(I32), in_=tab2_scales[:, 4 * q:4 * q + 4, :].bitcast(I32))
-        for a in range(NB):
-            nc.sync.dma_start(out=tab2_w[a][:], in_=tab2_words[a].rearrange("p t i -> p (t i)").bitcast(I32))
+        load_tab2(0)
+        nc.sync.dma_start(p1[:], pos1)
+        nc.sync.dma_start(p2[:], pos2)
+        load_cabin(0)
+        load_tab2(1)
+        load_gain(1)
         load_cabin(1)
         nc.sync.dma_start(out=exc_sb[:], in_=exc.rearrange("(a p) n -> p a n", p=P))
 
@@ -105,7 +111,7 @@ def tile_list_excursion_pair_ranks_kernel(tc, tab_words, tab_scales, offs, tab2_
         nc.scalar.copy(out=d, in_=s)
         v_s = keep.tile([P, S], U8, name="v_s", align_bytes=64)
         nc.vector.tensor_copy(out=v_s[:], in_=tab_s[:].indirect(idx[:]))
-        w1_q = [quantise(w1_woven[0], "w1q0")]
+        w1_q = [quantise(w1_woven[0], "w1q0", "tab_s")]
         VG = 256
         v_w = []
         for g in range(S // VG):
@@ -218,8 +224,7 @@ def tile_list_excursion_pair_ranks_kernel(tc, tab_words, tab_scales, offs, tab2_
 
         weave_on_scalar(x2_woven[0], x2_rows, 0)
         x1_q = [quantise(x1_woven[0], "x1q0")]
-        late_picks(0, P, "x2_late0")
-        late_picks(P, HN, "gain1")
+        late_picks(0, HN, "gain1")
         x1_q.append(quantise(x1_woven[1], "x1q1"))
         late_picks(HN, NP, "late")
         x2_q = [quantise(x2_woven[0], "x2q0")]

@@ -3,8 +3,8 @@ from contextlib import ExitStack
 import concourse.mybir as mybir
 from concourse.masks import make_identity
 
-K, H, T, S, T3, S2, NP = 512, 1024, 4096, 1024, 2048, 512, 512
-FLOPS = 2 * (2 * K * H * S + 2 * H * S2 * NP)
+K, H, T, S, T2, S2, N = 512, 1024, 4096, 1024, 2048, 512, 512
+FLOPS = 2 * (2 * K * H * S + 2 * H * S2 * N)
 
 F32 = mybir.dt.float32
 BF16 = mybir.dt.bfloat16
@@ -19,15 +19,28 @@ ALU = mybir.AluOpType
 
 P = 128
 PACK = 4
-KP = P * PACK
-NB = H // KP
-BANK = 512
+PASS = P * PACK
+BLOCKS = H // PASS
+CHUNKS = S // P
+TILES = S2 // P
+BANKS = 8
+QUADRANT = 32
+PER_COLUMN = 16
+ALIGN = 64
+
+WORD_PIECES = ((0, 256), (256, 512), (512, S))
+VECTOR_WEAVE = 256
+LATE_SPLIT = 384
+BENT_DEPTH, TERM_DEPTH = 8, 10
 
 
-def weave_views(dst, src, c0, c1):
-    d = dst[:, c0:c1, :].rearrange("p (c i) t -> p c t i", i=4)
-    s = src[:, :, c0:c1].rearrange("p t (c i) -> p c t i", i=4)
-    return d, s
+def weave_views(woven, rows, n0, c0, c1):
+    return (woven[:, n0 + c0:n0 + c1, :].rearrange("p (c i) t -> p c t i", i=4),
+            rows[:, :, c0:c1].rearrange("p t (c i) -> p c t i", i=4))
+
+
+def by_slot(bank):
+    return bank[:].rearrange("j (q t) -> j t q", t=PACK)
 
 
 def tile_list_excursion_pair_ranks_kernel(tc, tab_words, tab_scales, offs, tab2_words, tab2_scales, offs2,
@@ -41,21 +54,21 @@ def tile_list_excursion_pair_ranks_kernel(tc, tab_words, tab_scales, offs, tab2_
         tail = ctx.enter_context(tc.tile_pool(name="tail", bufs=1))
         psum = ctx.enter_context(tc.psum_pool(name="psum", bufs=1))
 
-        idx = lists.tile([P, S // 16], U16, name="idx")
-        idx2 = lists.tile([P, S2 // 16], U16, name="idx2")
-        p1 = lists.tile([P, NP // 16], U16, name="p1")
-        p2 = lists.tile([P, NP // 16], U16, name="p2")
+        idx = lists.tile([P, S // PER_COLUMN], U16, name="idx")
+        idx2 = lists.tile([P, S2 // PER_COLUMN], U16, name="idx2")
+        p1 = lists.tile([P, N // PER_COLUMN], U16, name="p1")
+        p2 = lists.tile([P, N // PER_COLUMN], U16, name="p2")
 
-        tab_w = keep.tile([P, T], I32, name="tab_w", tag="tab_w", align_bytes=64)
-        tab_s = keep.tile([P, T], U8, name="tab_s", tag="tab_s", align_bytes=64)
-        tab2_w = [keep.tile([P, T3], I32, name=f"tab2_w{a}") for a in range(NB)]
-        tab2_s = keep.tile([P, T3], U8, name="tab2_s")
-        w1_raw = [keep.tile([P, PACK, KP], F32, name=f"w1_raw{b}") for b in range(NB)]
-        w4_w = keep.tile([P, 2 * H], U8, name="w4_w", align_bytes=64)
-        w4_s = keep.tile([P, H], U8, name="w4_s", align_bytes=64)
-        gain_sb = [keep.tile([P, PACK], F32, name=f"gain{b}", tag=f"gain{b}", align_bytes=64) for b in range(NB)]
-        cabin_sb = [keep.tile([P, PACK, NP], F32, name=f"cabin{b}", tag=f"cabin{b}", align_bytes=64) for b in range(NB)]
-        exc_sb = keep.tile([P, S2 // P, NP], F32, name="exc_sb")
+        tab_w = keep.tile([P, T], I32, name="tab_w", tag="tab_w", align_bytes=ALIGN)
+        tab_s = keep.tile([P, T], U8, name="tab_s", tag="tab_s", align_bytes=ALIGN)
+        tab2_w = [keep.tile([P, T2], I32, name=f"tab2_w{a}") for a in range(BLOCKS)]
+        tab2_s = keep.tile([P, T2], U8, name="tab2_s")
+        w1_raw = [keep.tile([P, PACK, PASS], F32, name=f"w1_raw{b}") for b in range(BLOCKS)]
+        w4_w = keep.tile([P, 2 * H], U8, name="w4_w", align_bytes=ALIGN)
+        w4_s = keep.tile([P, H], U8, name="w4_s", align_bytes=ALIGN)
+        gain_sb = [keep.tile([P, PACK], F32, name=f"gain{b}", tag=f"gain{b}", align_bytes=ALIGN) for b in range(BLOCKS)]
+        cabin_sb = [keep.tile([P, PACK, N], F32, name=f"cabin{b}", align_bytes=ALIGN) for b in range(BLOCKS)]
+        exc_sb = keep.tile([P, TILES, N], F32, name="exc_sb")
         ident = keep.tile([P, P], F32, name="ident")
 
         nc.vector.memset(tab_s[:].bitcast(I32), 0)
@@ -63,199 +76,202 @@ def tile_list_excursion_pair_ranks_kernel(tc, tab_words, tab_scales, offs, tab2_
         nc.vector.memset(tab2_s[:].bitcast(I32), 0)
 
         def load_w1(b):
-            nc.sync.dma_start(out=w1_raw[b][:], in_=w1[:, b * KP:(b + 1) * KP].rearrange("(p j) c -> p j c", j=PACK))
+            nc.sync.dma_start(out=w1_raw[b][:], in_=w1[:, b * PASS:(b + 1) * PASS].rearrange("(p t) c -> p t c", t=PACK))
 
         def load_cabin(b):
-            nc.sync.dma_start(out=cabin_sb[b][:], in_=cabin[b * KP:(b + 1) * KP, :].rearrange("(p t) n -> p t n", t=PACK))
+            nc.sync.dma_start(out=cabin_sb[b][:], in_=cabin[b * PASS:(b + 1) * PASS, :].rearrange("(p t) n -> p t n", t=PACK))
 
         def load_gain(b):
-            nc.sync.dma_start(out=gain_sb[b][:], in_=gain[b * KP:(b + 1) * KP].rearrange("(p t) -> p t", t=PACK))
+            nc.sync.dma_start(out=gain_sb[b][:], in_=gain[b * PASS:(b + 1) * PASS].rearrange("(p t) -> p t", t=PACK))
 
-        def load_tab2(a):
-            nc.sync.dma_start(out=tab2_w[a][:], in_=tab2_words[a].rearrange("p t i -> p (t i)").bitcast(I32))
+        def load_scale_rows(tile, rows):
+            for r in range(4):
+                nc.sync.dma_start(out=tile[r:P:QUADRANT, :].bitcast(I32), in_=rows[r:16:4, :].bitcast(I32))
 
         nc.sync.dma_start(idx[:], offs)
         load_w1(0)
-        for q in range(4):
-            nc.sync.dma_start(out=tab_s[q:P:32, :].bitcast(I32), in_=tab_scales[0, q:16:4, :].bitcast(I32))
+        load_scale_rows(tab_s, tab_scales[0])
         nc.sync.dma_start(out=tab_w[:], in_=tab_words[0].rearrange("p t i -> p (t i)").bitcast(I32))
         nc.sync.dma_start(out=w4_w[:].bitcast(I32), in_=w4_words[0].bitcast(I32))
-        for q in range(4):
-            nc.sync.dma_start(out=w4_s[q:P:32, :].bitcast(I32), in_=w4_scales[0, q:16:4, :].bitcast(I32))
+        load_scale_rows(w4_s, w4_scales[0])
         make_identity(nc, ident[:])
         load_w1(1)
         load_gain(0)
         nc.sync.dma_start(idx2[:], offs2)
-        for q in range(4):
-            nc.sync.dma_start(out=tab2_s[32 * q:32 * q + 4 * NB, :].bitcast(I32), in_=tab2_scales[:, 4 * q:4 * q + 4, :].bitcast(I32))
-        load_tab2(0)
+        for q in range(P // QUADRANT):
+            nc.sync.dma_start(out=tab2_s[QUADRANT * q:QUADRANT * q + 4 * BLOCKS, :].bitcast(I32),
+                              in_=tab2_scales[:, 4 * q:4 * q + 4, :].bitcast(I32))
+        for a in range(BLOCKS):
+            nc.sync.dma_start(out=tab2_w[a][:], in_=tab2_words[a].rearrange("p t i -> p (t i)").bitcast(I32))
         nc.sync.dma_start(p1[:], pos1)
         nc.sync.dma_start(p2[:], pos2)
         load_cabin(0)
-        load_tab2(1)
         load_gain(1)
         load_cabin(1)
         nc.sync.dma_start(out=exc_sb[:], in_=exc.rearrange("(a p) n -> p a n", p=P))
 
-        def woven_tile(name):
-            return ring.tile([P, KP, PACK], BF16, name=name, tag="woven", bufs=1, align_bytes=64)
-
-        def quantise(woven, name, tag=None):
-            codes = keep.tile([P, KP], U32, name=name + "_codes", tag=tag or name, align_bytes=64)
-            scales = keep.tile([P, KP], U8, name=name + "_scales", align_bytes=64)
+        def quantise(woven, name, tag):
+            codes = keep.tile([P, PASS], U32, name=name + "_codes", tag=tag, align_bytes=ALIGN)
+            scales = keep.tile([P, PASS], U8, name=name + "_scales", align_bytes=ALIGN)
             nc.vector.quantize_mx(out=codes[:].bitcast(FP8X4), scales=scales[:], in_=woven[:].rearrange("p n t -> p (n t)"))
             return codes, scales
 
-        w1_woven = [woven_tile("w1_woven0")]
-        d, s = weave_views(w1_woven[0], w1_raw[0], 0, KP)
-        nc.scalar.copy(out=d, in_=s)
-        v_s = keep.tile([P, S], U8, name="v_s", align_bytes=64)
+        w1_woven = [ring.tile([P, PASS, PACK], BF16, name="w1_woven0", align_bytes=ALIGN)]
+        dst, src = weave_views(w1_woven[0], w1_raw[0], 0, 0, PASS)
+        nc.scalar.copy(out=dst, in_=src)
+        v_s = keep.tile([P, S], U8, name="v_s", align_bytes=ALIGN)
         nc.vector.tensor_copy(out=v_s[:], in_=tab_s[:].indirect(idx[:]))
         w1_q = [quantise(w1_woven[0], "w1q0", "tab_s")]
-        VG = 256
         v_w = []
-        for g in range(S // VG):
-            piece = keep.tile([P, VG], U32, name=f"v_w{g}", tag=f"v_w{g}", align_bytes=64)
-            nc.vector.tensor_copy(out=piece[:], in_=tab_w[:].bitcast(U32).indirect(idx[:, g * VG // 16:(g + 1) * VG // 16]))
-            v_w.append(piece)
-        w1_woven.append(keep.tile([P, KP, PACK], BF16, name="w1_woven1", tag="tab_w", align_bytes=64))
-        nc.gpsimd.tensor_scalar(out=w1_woven[1][:], in0=w1_raw[1][:].rearrange("p j c -> p c j"), scalar1=1.0, scalar2=0.0, op0=ALU.mult, op1=ALU.add)
-
-        def by_slot(bank):
-            return bank[:].rearrange("j (q t) -> j t q", t=PACK)
+        for j0, j1 in WORD_PIECES:
+            piece = keep.tile([P, j1 - j0], U32, name=f"v_w{j0}", tag=f"v_w{j0}", align_bytes=ALIGN)
+            nc.vector.tensor_copy(out=piece[:], in_=tab_w[:].bitcast(U32).indirect(idx[:, j0 // PER_COLUMN:j1 // PER_COLUMN]))
+            v_w.extend(piece[:, c:c + P] for c in range(0, j1 - j0, P))
+        last_piece_tag = f"v_w{WORD_PIECES[-1][0]}"
+        w1_woven.append(keep.tile([P, PASS, PACK], BF16, name="w1_woven1", tag="tab_w", align_bytes=ALIGN))
+        nc.gpsimd.tensor_scalar(out=w1_woven[1][:], in0=w1_raw[1][:].rearrange("p t c -> p c t"), scalar1=1.0, scalar2=0.0,
+                                op0=ALU.mult, op1=ALU.add)
 
         def bank_tile(k, name):
-            return psum.tile([P, BANK], F32, name=name, tag=f"bank{k}")
+            return psum.tile([P, PASS], F32, name=name, tag=f"bank{k}")
 
-        def unit(b, jc, add_on_vector, banks):
-            words = v_w[jc * P // VG][:, jc * P % VG:jc * P % VG + P].bitcast(FP8X4)
-            scale = v_s[:, jc * P:(jc + 1) * P]
-            a_bank = bank_tile((2 * jc) % banks, "a_bank")
-            nc.tensor.matmul_mx(out=a_bank[:], lhsT=words, lhsT_scale=scale, rhs=w1_q[b][0][:].bitcast(FP8X4),
-                                rhs_scale=w1_q[b][1][:], start=True, stop=True)
-            b_bank = bank_tile((2 * jc + 1) % banks, "b_bank")
-            nc.tensor.matmul_mx(out=b_bank[:], lhsT=words, lhsT_scale=scale,
-                                rhs=w4_w[:, 2 * b * KP:2 * (b + 1) * KP].bitcast(FP4X4),
-                                rhs_scale=w4_s[:, b * KP:(b + 1) * KP], start=True, stop=True)
-            if jc == 7 and b == 0:
-                bent = shared.tile([P, PACK, P], F32, name="bent_last", offset=0, align_bytes=64)
-            elif jc == 7:
-                bent = keep.tile([P, PACK, P], F32, name="bent", tag=f"last{b}", align_bytes=64)
-            else:
-                bent = ring.tile([P, PACK, P], F32, name="bent", tag="bent", bufs=8)
-            nc.scalar.activation(out=bent[:], in_=by_slot(a_bank), func=ACT.Tanh)
-            other = ring.tile([P, PACK, P], F32, name="other", tag="other", bufs=10)
-            if add_on_vector:
-                nc.vector.tensor_tensor(out=other[:], in0=by_slot(b_bank), in1=bent[:], op=ALU.add)
-                return [other]
-            nc.scalar.copy(out=other[:], in_=by_slot(b_bank))
-            return [other, bent]
-
-        def turn(parts, t, half, k):
-            bank = bank_tile(k, "h_bank")
-            for c in range(4):
-                terms = parts[4 * half + c]
-                for i, term in enumerate(terms):
-                    nc.tensor.matmul(out=bank[:, c * P:(c + 1) * P], lhsT=term[:, t, :], rhs=ident[:], is_transpose=True,
-                                     start=(i == 0), stop=(i == len(terms) - 1))
+        def product(chunk, k, rhs, rhs_scale):
+            bank = bank_tile(k, "sum_bank")
+            nc.tensor.matmul_mx(out=bank[:], lhsT=v_w[chunk].bitcast(FP8X4), lhsT_scale=v_s[:, chunk * P:(chunk + 1) * P],
+                                rhs=rhs, rhs_scale=rhs_scale, start=True, stop=True)
             return bank
 
-        def land(h, bank, b, t, half):
-            nc.scalar.activation(out=h[:, half * BANK:(half + 1) * BANK], in_=bank[:], func=ACT.Copy,
-                                 scale=gain_sb[b][:, t:t + 1])
+        def w1_product(b, chunk, banks):
+            return product(chunk, (2 * chunk) % banks, w1_q[b][0][:].bitcast(FP8X4), w1_q[b][1][:])
 
-        x1_rows = [keep.tile([P, PACK, NP], F32, name=f"x1_rows{b}") for b in range(NB)]
+        def w4_product(b, chunk, banks):
+            return product(chunk, (2 * chunk + 1) % banks, w4_w[:, 2 * b * PASS:2 * (b + 1) * PASS].bitcast(FP4X4),
+                           w4_s[:, b * PASS:(b + 1) * PASS])
 
-        def pick1(h, b, t):
-            nc.vector.tensor_tensor(out=x1_rows[b][:, t, :], in0=h[:].indirect(p1[:]), in1=cabin_sb[b][:, t, :], op=ALU.mult)
+        def bend(b, chunk, bank):
+            if (b, chunk) == (0, CHUNKS - 2):
+                bent = shared.tile([P, PACK, P], F32, name="bent_shared", offset=0, align_bytes=ALIGN)
+            elif (b, chunk) == (1, CHUNKS - 1):
+                bent = keep.tile([P, PACK, P], F32, name="bent_last", tag="bent_last", align_bytes=ALIGN)
+            else:
+                bent = ring.tile([P, PACK, P], F32, name="bent", tag="bent", bufs=BENT_DEPTH)
+            nc.scalar.activation(out=bent[:], in_=by_slot(bank), func=ACT.Tanh)
+            return bent
 
-        def weave_on_gpsimd(woven, rows):
-            nc.gpsimd.tensor_scalar(out=woven[:], in0=rows[:].rearrange("p t n -> p n t"), scalar1=1.0, scalar2=0.0, op0=ALU.mult, op1=ALU.add)
-            return woven
+        def term_tile():
+            return ring.tile([P, PACK, P], F32, name="term", tag="term", bufs=TERM_DEPTH)
 
-        hs = [[keep.tile([P, S], F32, name=f"h{b}{t}") for t in range(PACK)] for b in range(NB)]
+        def two_terms(chunk):
+            w1_bank = w1_product(1, chunk, BANKS // 2)
+            w4_bank = w4_product(1, chunk, BANKS // 2)
+            bent = bend(1, chunk, w1_bank)
+            plain = term_tile()
+            nc.scalar.copy(out=plain[:], in_=by_slot(w4_bank))
+            return [plain, bent]
 
-        def rows_of(b, t, parts, first_bank):
+        x1_rows = [keep.tile([P, PACK, N], F32, name=f"x1_rows{b}") for b in range(BLOCKS)]
+        h = [[keep.tile([P, S], F32, name=f"h{b}{t}") for t in range(PACK)] for b in range(BLOCKS)]
+
+        def make_rows(b, t, terms, first_bank):
             for half in range(2):
-                land(hs[b][t], turn(parts, t, half, first_bank + half), b, t, half)
+                bank = bank_tile(first_bank + half, "h_bank")
+                for c in range(CHUNKS // 2):
+                    chunk_terms = terms[CHUNKS // 2 * half + c]
+                    for i, term in enumerate(chunk_terms):
+                        nc.tensor.matmul(out=bank[:, c * P:(c + 1) * P], lhsT=term[:, t, :], rhs=ident[:], is_transpose=True,
+                                         start=(i == 0), stop=(i == len(chunk_terms) - 1))
+                nc.scalar.activation(out=h[b][t][:, half * PASS:(half + 1) * PASS], in_=bank[:], func=ACT.Copy,
+                                     scale=gain_sb[b][:, t:t + 1])
 
-        parts0 = [unit(0, jc, True, 8) for jc in range(6)]
-        w1_q.append(quantise(w1_woven[1], "w1q1"))
-        parts0 = parts0 + [unit(0, jc, True, 8) for jc in range(6, 8)]
-        v2_s = shared.tile([P, S2], U8, name="v2_s", offset=0, align_bytes=64)
+        def pick_holders(b, t):
+            nc.vector.tensor_tensor(out=x1_rows[b][:, t, :], in0=h[b][t][:].indirect(p1[:]), in1=cabin_sb[b][:, t, :],
+                                    op=ALU.mult)
+
+        terms0 = []
+        for pair in range(CHUNKS // 2):
+            if pair == CHUNKS // 2 - 1:
+                w1_q.append(quantise(w1_woven[1], "w1q1", "w1q1"))
+            chunks = (2 * pair, 2 * pair + 1)
+            bents = [bend(0, chunk, w1_product(0, chunk, BANKS)) for chunk in chunks]
+            for chunk, bent in zip(chunks, bents):
+                summed = term_tile()
+                nc.vector.tensor_tensor(out=summed[:], in0=by_slot(w4_product(0, chunk, BANKS)), in1=bent[:], op=ALU.add)
+                terms0.append([summed])
+
+        v2_s = shared.tile([P, S2], U8, name="v2_s", offset=0, align_bytes=ALIGN)
         nc.vector.tensor_copy(out=v2_s[:], in_=tab2_s[:].indirect(idx2[:]))
-        v2_w = shared.tile([P, NB, S2], U32, name="v2_w", offset=S2, align_bytes=64)
-        for a in range(NB):
+        v2_w = shared.tile([P, BLOCKS, S2], U32, name="v2_w", offset=S2, align_bytes=ALIGN)
+        for a in range(BLOCKS):
             nc.vector.tensor_copy(out=v2_w[:, a, :], in_=tab2_w[a][:].bitcast(U32).indirect(idx2[:]))
-        parts1 = []
-        x2_rows = keep.tile([P, PACK, NP], BF16, name="x2_rows0")
-        for t in range(PACK):
-            rows_of(0, t, parts0, 4 + 2 * (t % 2))
-            pick1(hs[0][t], 0, t)
-            nc.vector.tensor_copy(out=x2_rows[:, t, :], in_=hs[0][t][:].indirect(p2[:]))
-            parts1.append(unit(1, t, False, 4))
-        x1_woven = [keep.tile([P, KP, PACK], BF16, name="x1_woven0", tag="v_w3", align_bytes=64)]
-        d, s = weave_views(x1_woven[0], x1_rows[0], 0, 256)
-        nc.vector.tensor_copy(out=d, in_=s)
-        for jc in range(PACK, 8):
-            parts1.append(unit(1, jc, False, 4))
-        for t in range(PACK):
-            rows_of(1, t, parts1, (4 + 2 * t) % 8)
-            pick1(hs[1][t], 1, t)
 
-        def weave_on_scalar(woven, rows, n0, first=0):
+        terms1 = []
+        x2_rows = keep.tile([P, PACK, N], BF16, name="x2_rows")
+        for t in range(PACK):
+            make_rows(0, t, terms0, BANKS // 2 + 2 * (t % 2))
+            pick_holders(0, t)
+            nc.vector.tensor_copy(out=x2_rows[:, t, :], in_=h[0][t][:].indirect(p2[:]))
+            terms1.append(two_terms(t))
+        x1_woven = [keep.tile([P, N, PACK], BF16, name="x1_woven0", tag=last_piece_tag, align_bytes=ALIGN)]
+        dst, src = weave_views(x1_woven[0], x1_rows[0], 0, 0, VECTOR_WEAVE)
+        nc.vector.tensor_copy(out=dst, in_=src)
+        for chunk in range(PACK, CHUNKS):
+            terms1.append(two_terms(chunk))
+        for t in range(PACK):
+            make_rows(1, t, terms1, (BANKS // 2 + 2 * t) % BANKS)
+            pick_holders(1, t)
+
+        def weave_on_scalar(woven, rows, n0, first):
             for c0 in range(first, rows.shape[2], P):
-                dd = woven[:, n0 + c0:n0 + c0 + P, :].rearrange("p (c i) t -> p c t i", i=4)
-                ss = rows[:, :, c0:c0 + P].rearrange("p t (c i) -> p c t i", i=4)
-                nc.scalar.copy(out=dd, in_=ss)
-            return woven
+                to, source = weave_views(woven, rows, n0, c0, c0 + P)
+                nc.scalar.copy(out=to, in_=source)
 
-        weave_on_scalar(x1_woven[0], x1_rows[0], 0, 256)
-        x1_woven.append(weave_on_scalar(keep.tile([P, KP, PACK], BF16, name="x1_woven1", tag="late", align_bytes=64), x1_rows[1], 0))
-        HN = 384
-        x2_woven = [keep.tile([P, KP, PACK], BF16, name="x2_woven0", tag="last1", align_bytes=64),
-                    tail.tile([P, KP, PACK], BF16, name="x2_woven1", offset=0, align_bytes=64)]
+        weave_on_scalar(x1_woven[0], x1_rows[0], 0, VECTOR_WEAVE)
+        x1_woven.append(keep.tile([P, N, PACK], BF16, name="x1_woven1", tag="x1_woven1", align_bytes=ALIGN))
+        weave_on_scalar(x1_woven[1], x1_rows[1], 0, 0)
+        x2_woven = [keep.tile([P, N, PACK], BF16, name="x2_woven0", tag="bent_last", align_bytes=ALIGN),
+                    tail.tile([P, N, PACK], BF16, name="x2_woven1", offset=0, align_bytes=ALIGN)]
 
-        def late_picks(n0, n1, tag):
-            rows = keep.tile([P, PACK, n1 - n0], BF16, name=f"x2_late{n0}", tag=tag, align_bytes=64)
+        def pick_late_companions(n0, n1, tag):
+            rows = keep.tile([P, PACK, n1 - n0], BF16, name=f"x2_late{n0}", tag=tag, align_bytes=ALIGN)
             for t in range(PACK):
-                nc.vector.tensor_copy(out=rows[:, t, :], in_=hs[1][t][:].indirect(p2[:, n0 // 16:n1 // 16]))
-            weave_on_scalar(x2_woven[1], rows, n0)
+                nc.vector.tensor_copy(out=rows[:, t, :], in_=h[1][t][:].indirect(p2[:, n0 // PER_COLUMN:n1 // PER_COLUMN]))
+            weave_on_scalar(x2_woven[1], rows, n0, 0)
 
-        weave_on_scalar(x2_woven[0], x2_rows, 0)
-        x1_q = [quantise(x1_woven[0], "x1q0")]
-        late_picks(0, HN, "gain1")
-        x1_q.append(quantise(x1_woven[1], "x1q1"))
-        late_picks(HN, NP, "late")
-        x2_q = [quantise(x2_woven[0], "x2q0")]
+        weave_on_scalar(x2_woven[0], x2_rows, 0, 0)
+        x1_q = [quantise(x1_woven[0], "x1q0", "x1q0")]
+        pick_late_companions(0, LATE_SPLIT, "gain1")
+        x1_q.append(quantise(x1_woven[1], "x1q1", "x1q1"))
+        pick_late_companions(LATE_SPLIT, N, "x1_woven1")
+        x2_q = [quantise(x2_woven[0], "x2q0", "x2q0")]
 
-        def score_pass(bank, m, a, xq):
+        def score_pass(bank, m, a, x_q):
             nc.tensor.matmul_mx(out=bank[:], lhsT=v2_w[:, a, m * P:(m + 1) * P].bitcast(FP8X4),
-                                lhsT_scale=v2_s[4 * a:P, m * P:(m + 1) * P], rhs=xq[0][:].bitcast(FP8X4), rhs_scale=xq[1][:],
-                                start=(a == 0), stop=(a == NB - 1))
+                                lhsT_scale=v2_s[4 * a:P, m * P:(m + 1) * P], rhs=x_q[0][:].bitcast(FP8X4), rhs_scale=x_q[1][:],
+                                start=(a == 0), stop=(a == BLOCKS - 1))
 
-        MT = S2 // P
-        e1 = [bank_tile(4 + m, f"e1_{m}") for m in range(MT)]
-        e2 = [bank_tile(m, f"e2_{m}") for m in range(MT)]
-        for a in range(NB):
-            for m in range(MT):
+        e1 = [bank_tile(TILES + m, f"e1_{m}") for m in range(TILES)]
+        e2 = [bank_tile(m, f"e2_{m}") for m in range(TILES)]
+        for a in range(BLOCKS):
+            for m in range(TILES):
                 score_pass(e1[m], m, a, x1_q[a])
-        for m in range(MT):
+        for m in range(TILES):
             score_pass(e2[m], m, 0, x2_q[0])
+
         def shift(m, tile):
             nc.vector.tensor_tensor(out=tile[:], in0=e1[m][:], in1=exc_sb[:, m, :], op=ALU.add)
             return tile
 
-        shifted = [shift(0, keep.tile([P, NP], F32, name="shifted0")),
-                   shift(1, keep.tile([P, NP], F32, name="shifted1", tag="last1", align_bytes=64))]
-        x2_q.append(quantise(x2_woven[1], "x2q1"))
-        e1_last = keep.tile([P, NP], F32, name="e1_last")
-        nc.scalar.copy(out=e1_last[:], in_=e1[3][:])
-        shifted.append(shift(2, tail.tile([P, NP], F32, name="shifted2", offset=0, align_bytes=64)))
-        shifted.append(tail.tile([P, NP], F32, name="shifted3", offset=4 * NP, align_bytes=64))
-        nc.gpsimd.tensor_tensor(out=shifted[3][:], in0=e1_last[:], in1=exc_sb[:, 3, :], op=ALU.add)
-        for m in range(MT):
+        last = TILES - 1
+        result = [shift(0, keep.tile([P, N], F32, name="result0")),
+                  shift(1, keep.tile([P, N], F32, name="result1", tag="bent_last", align_bytes=ALIGN))]
+        x2_q.append(quantise(x2_woven[1], "x2q1", "x2q1"))
+        e1_last = keep.tile([P, N], F32, name="e1_last")
+        nc.scalar.copy(out=e1_last[:], in_=e1[last][:])
+        result.append(shift(2, tail.tile([P, N], F32, name="result2", offset=0, align_bytes=ALIGN)))
+        result.append(tail.tile([P, N], F32, name="result3", offset=4 * N, align_bytes=ALIGN))
+        nc.gpsimd.tensor_tensor(out=result[last][:], in0=e1_last[:], in1=exc_sb[:, last, :], op=ALU.add)
+        for m in range(TILES):
             score_pass(e2[m], m, 1, x2_q[1])
-        for m in range(MT):
-            nc.vector.tensor_tensor(out=shifted[m][:], in0=e2[m][:], in1=shifted[m][:], op=ALU.mult)
-            nc.sync.dma_start(out=out[m * P:(m + 1) * P, :], in_=shifted[m][:])
+        for m in range(TILES):
+            nc.vector.tensor_tensor(out=result[m][:], in0=e2[m][:], in1=result[m][:], op=ALU.mult)
+            nc.sync.dma_start(out=out[m * P:(m + 1) * P, :], in_=result[m][:])

from contextlib import ExitStack

import concourse.mybir as mybir
from concourse.masks import make_identity

K, H, T, S, T2, S2, N = 512, 1024, 4096, 1024, 2048, 512, 512
FLOPS = 2 * (2 * K * H * S + 2 * H * S2 * N)

F32 = mybir.dt.float32
BF16 = mybir.dt.bfloat16
I32 = mybir.dt.int32
U32 = mybir.dt.uint32
U16 = mybir.dt.uint16
U8 = mybir.dt.uint8
FP8X4 = mybir.dt.float8_e4m3fn_x4
FP4X4 = mybir.dt.float4_e2m1fn_x4
ACT = mybir.ActivationFunctionType
ALU = mybir.AluOpType

P = 128
PACK = 4
PASS = P * PACK
BLOCKS = H // PASS
CHUNKS = S // P
TILES = S2 // P
BANKS = 8
QUADRANT = 32
PER_COLUMN = 16
ALIGN = 64

WORD_PIECES = ((0, 256), (256, 512), (512, S))
VECTOR_WEAVE = 256
LATE_SPLIT = 384
BENT_DEPTH, TERM_DEPTH = 8, 10


def weave_views(woven, rows, n0, c0, c1):
    return (woven[:, n0 + c0:n0 + c1, :].rearrange("p (c i) t -> p c t i", i=4),
            rows[:, :, c0:c1].rearrange("p t (c i) -> p c t i", i=4))


def by_slot(bank):
    return bank[:].rearrange("j (q t) -> j t q", t=PACK)


def tile_list_excursion_pair_ranks_kernel(tc, tab_words, tab_scales, offs, tab2_words, tab2_scales, offs2,
                                                    pos1, pos2, w1, w4_words, w4_scales, gain, cabin, exc, out):
    nc = tc.nc
    with ExitStack() as ctx:
        lists = ctx.enter_context(tc.tile_pool(name="lists", bufs=1))
        keep = ctx.enter_context(tc.tile_pool(name="keep", bufs=1))
        ring = ctx.enter_context(tc.tile_pool(name="ring", bufs=1))
        shared = ctx.enter_context(tc.tile_pool(name="shared", bufs=1))
        tail = ctx.enter_context(tc.tile_pool(name="tail", bufs=1))
        psum = ctx.enter_context(tc.psum_pool(name="psum", bufs=1))

        idx = lists.tile([P, S // PER_COLUMN], U16, name="idx")
        idx2 = lists.tile([P, S2 // PER_COLUMN], U16, name="idx2")
        p1 = lists.tile([P, N // PER_COLUMN], U16, name="p1")
        p2 = lists.tile([P, N // PER_COLUMN], U16, name="p2")

        tab_w = keep.tile([P, T], I32, name="tab_w", tag="tab_w", align_bytes=ALIGN)
        tab_s = keep.tile([P, T], U8, name="tab_s", tag="tab_s", align_bytes=ALIGN)
        tab2_w = [keep.tile([P, T2], I32, name=f"tab2_w{a}") for a in range(BLOCKS)]
        tab2_s = keep.tile([P, T2], U8, name="tab2_s")
        w1_raw = [keep.tile([P, PACK, PASS], F32, name=f"w1_raw{b}") for b in range(BLOCKS)]
        w4_w = keep.tile([P, 2 * H], U8, name="w4_w", align_bytes=ALIGN)
        w4_s = keep.tile([P, H], U8, name="w4_s", align_bytes=ALIGN)
        gain_sb = [keep.tile([P, PACK], F32, name=f"gain{b}", tag=f"gain{b}", align_bytes=ALIGN) for b in range(BLOCKS)]
        cabin_sb = [keep.tile([P, PACK, N], F32, name=f"cabin{b}", align_bytes=ALIGN) for b in range(BLOCKS)]
        exc_sb = keep.tile([P, TILES, N], F32, name="exc_sb")
        ident = keep.tile([P, P], F32, name="ident")

        nc.vector.memset(tab_s[:].bitcast(I32), 0)
        nc.gpsimd.memset(w4_s[:].bitcast(I32), 0)
        nc.vector.memset(tab2_s[:].bitcast(I32), 0)

        def load_w1(b):
            nc.sync.dma_start(out=w1_raw[b][:], in_=w1[:, b * PASS:(b + 1) * PASS].rearrange("(p t) c -> p t c", t=PACK))

        def load_cabin(b):
            nc.sync.dma_start(out=cabin_sb[b][:], in_=cabin[b * PASS:(b + 1) * PASS, :].rearrange("(p t) n -> p t n", t=PACK))

        def load_gain(b):
            nc.sync.dma_start(out=gain_sb[b][:], in_=gain[b * PASS:(b + 1) * PASS].rearrange("(p t) -> p t", t=PACK))

        def load_scale_rows(tile, rows):
            for r in range(4):
                nc.sync.dma_start(out=tile[r:P:QUADRANT, :].bitcast(I32), in_=rows[r:16:4, :].bitcast(I32))

        nc.sync.dma_start(idx[:], offs)
        load_w1(0)
        load_scale_rows(tab_s, tab_scales[0])
        nc.sync.dma_start(out=tab_w[:], in_=tab_words[0].rearrange("p t i -> p (t i)").bitcast(I32))
        nc.sync.dma_start(out=w4_w[:].bitcast(I32), in_=w4_words[0].bitcast(I32))
        load_scale_rows(w4_s, w4_scales[0])
        make_identity(nc, ident[:])
        load_w1(1)
        load_gain(0)
        nc.sync.dma_start(idx2[:], offs2)
        for q in range(P // QUADRANT):
            nc.sync.dma_start(out=tab2_s[QUADRANT * q:QUADRANT * q + 4 * BLOCKS, :].bitcast(I32),
                              in_=tab2_scales[:, 4 * q:4 * q + 4, :].bitcast(I32))
        for a in range(BLOCKS):
            nc.sync.dma_start(out=tab2_w[a][:], in_=tab2_words[a].rearrange("p t i -> p (t i)").bitcast(I32))
        nc.sync.dma_start(p1[:], pos1)
        nc.sync.dma_start(p2[:], pos2)
        load_cabin(0)
        load_gain(1)
        load_cabin(1)
        nc.sync.dma_start(out=exc_sb[:], in_=exc.rearrange("(a p) n -> p a n", p=P))

        def quantise(woven, name, tag):
            codes = keep.tile([P, PASS], U32, name=name + "_codes", tag=tag, align_bytes=ALIGN)
            scales = keep.tile([P, PASS], U8, name=name + "_scales", align_bytes=ALIGN)
            nc.vector.quantize_mx(out=codes[:].bitcast(FP8X4), scales=scales[:], in_=woven[:].rearrange("p n t -> p (n t)"))
            return codes, scales

        w1_woven = [ring.tile([P, PASS, PACK], BF16, name="w1_woven0", align_bytes=ALIGN)]
        dst, src = weave_views(w1_woven[0], w1_raw[0], 0, 0, PASS)
        nc.scalar.copy(out=dst, in_=src)
        v_s = keep.tile([P, S], U8, name="v_s", align_bytes=ALIGN)
        nc.vector.tensor_copy(out=v_s[:], in_=tab_s[:].indirect(idx[:]))
        w1_q = [quantise(w1_woven[0], "w1q0", "tab_s")]
        v_w = []
        for j0, j1 in WORD_PIECES:
            piece = keep.tile([P, j1 - j0], U32, name=f"v_w{j0}", tag=f"v_w{j0}", align_bytes=ALIGN)
            nc.vector.tensor_copy(out=piece[:], in_=tab_w[:].bitcast(U32).indirect(idx[:, j0 // PER_COLUMN:j1 // PER_COLUMN]))
            v_w.extend(piece[:, c:c + P] for c in range(0, j1 - j0, P))
        last_piece_tag = f"v_w{WORD_PIECES[-1][0]}"
        w1_woven.append(keep.tile([P, PASS, PACK], BF16, name="w1_woven1", tag="tab_w", align_bytes=ALIGN))
        nc.gpsimd.tensor_scalar(out=w1_woven[1][:], in0=w1_raw[1][:].rearrange("p t c -> p c t"), scalar1=1.0, scalar2=0.0,
                                op0=ALU.mult, op1=ALU.add)

        def bank_tile(k, name):
            return psum.tile([P, PASS], F32, name=name, tag=f"bank{k}")

        def product(chunk, k, rhs, rhs_scale):
            bank = bank_tile(k, "sum_bank")
            nc.tensor.matmul_mx(out=bank[:], lhsT=v_w[chunk].bitcast(FP8X4), lhsT_scale=v_s[:, chunk * P:(chunk + 1) * P],
                                rhs=rhs, rhs_scale=rhs_scale, start=True, stop=True)
            return bank

        def w1_product(b, chunk, banks):
            return product(chunk, (2 * chunk) % banks, w1_q[b][0][:].bitcast(FP8X4), w1_q[b][1][:])

        def w4_product(b, chunk, banks):
            return product(chunk, (2 * chunk + 1) % banks, w4_w[:, 2 * b * PASS:2 * (b + 1) * PASS].bitcast(FP4X4),
                           w4_s[:, b * PASS:(b + 1) * PASS])

        def bend(b, chunk, bank):
            if (b, chunk) == (0, CHUNKS - 2):
                bent = shared.tile([P, PACK, P], F32, name="bent_shared", offset=0, align_bytes=ALIGN)
            elif (b, chunk) == (1, CHUNKS - 1):
                bent = keep.tile([P, PACK, P], F32, name="bent_last", tag="bent_last", align_bytes=ALIGN)
            else:
                bent = ring.tile([P, PACK, P], F32, name="bent", tag="bent", bufs=BENT_DEPTH)
            nc.scalar.activation(out=bent[:], in_=by_slot(bank), func=ACT.Tanh)
            return bent

        def term_tile():
            return ring.tile([P, PACK, P], F32, name="term", tag="term", bufs=TERM_DEPTH)

        def two_terms(chunk):
            w1_bank = w1_product(1, chunk, BANKS // 2)
            w4_bank = w4_product(1, chunk, BANKS // 2)
            bent = bend(1, chunk, w1_bank)
            plain = term_tile()
            nc.scalar.copy(out=plain[:], in_=by_slot(w4_bank))
            return [plain, bent]

        x1_rows = [keep.tile([P, PACK, N], F32, name=f"x1_rows{b}") for b in range(BLOCKS)]
        h = [[keep.tile([P, S], F32, name=f"h{b}{t}") for t in range(PACK)] for b in range(BLOCKS)]

        def make_rows(b, t, terms, first_bank):
            for half in range(2):
                bank = bank_tile(first_bank + half, "h_bank")
                for c in range(CHUNKS // 2):
                    chunk_terms = terms[CHUNKS // 2 * half + c]
                    for i, term in enumerate(chunk_terms):
                        nc.tensor.matmul(out=bank[:, c * P:(c + 1) * P], lhsT=term[:, t, :], rhs=ident[:], is_transpose=True,
                                         start=(i == 0), stop=(i == len(chunk_terms) - 1))
                nc.scalar.activation(out=h[b][t][:, half * PASS:(half + 1) * PASS], in_=bank[:], func=ACT.Copy,
                                     scale=gain_sb[b][:, t:t + 1])

        def pick_holders(b, t):
            nc.vector.tensor_tensor(out=x1_rows[b][:, t, :], in0=h[b][t][:].indirect(p1[:]), in1=cabin_sb[b][:, t, :],
                                    op=ALU.mult)

        terms0 = []
        for pair in range(CHUNKS // 2):
            if pair == CHUNKS // 2 - 1:
                w1_q.append(quantise(w1_woven[1], "w1q1", "w1q1"))
            chunks = (2 * pair, 2 * pair + 1)
            bents = [bend(0, chunk, w1_product(0, chunk, BANKS)) for chunk in chunks]
            for chunk, bent in zip(chunks, bents):
                summed = term_tile()
                nc.vector.tensor_tensor(out=summed[:], in0=by_slot(w4_product(0, chunk, BANKS)), in1=bent[:], op=ALU.add)
                terms0.append([summed])

        v2_s = shared.tile([P, S2], U8, name="v2_s", offset=0, align_bytes=ALIGN)
        nc.vector.tensor_copy(out=v2_s[:], in_=tab2_s[:].indirect(idx2[:]))
        v2_w = shared.tile([P, BLOCKS, S2], U32, name="v2_w", offset=S2, align_bytes=ALIGN)
        for a in range(BLOCKS):
            nc.vector.tensor_copy(out=v2_w[:, a, :], in_=tab2_w[a][:].bitcast(U32).indirect(idx2[:]))

        terms1 = []
        x2_rows = keep.tile([P, PACK, N], BF16, name="x2_rows")
        for t in range(PACK):
            make_rows(0, t, terms0, BANKS // 2 + 2 * (t % 2))
            pick_holders(0, t)
            nc.vector.tensor_copy(out=x2_rows[:, t, :], in_=h[0][t][:].indirect(p2[:]))
            terms1.append(two_terms(t))
        x1_woven = [keep.tile([P, N, PACK], BF16, name="x1_woven0", tag=last_piece_tag, align_bytes=ALIGN)]
        dst, src = weave_views(x1_woven[0], x1_rows[0], 0, 0, VECTOR_WEAVE)
        nc.vector.tensor_copy(out=dst, in_=src)
        for chunk in range(PACK, CHUNKS):
            terms1.append(two_terms(chunk))
        for t in range(PACK):
            make_rows(1, t, terms1, (BANKS // 2 + 2 * t) % BANKS)
            pick_holders(1, t)

        def weave_on_scalar(woven, rows, n0, first):
            for c0 in range(first, rows.shape[2], P):
                to, source = weave_views(woven, rows, n0, c0, c0 + P)
                nc.scalar.copy(out=to, in_=source)

        weave_on_scalar(x1_woven[0], x1_rows[0], 0, VECTOR_WEAVE)
        x1_woven.append(keep.tile([P, N, PACK], BF16, name="x1_woven1", tag="x1_woven1", align_bytes=ALIGN))
        weave_on_scalar(x1_woven[1], x1_rows[1], 0, 0)
        x2_woven = [keep.tile([P, N, PACK], BF16, name="x2_woven0", tag="bent_last", align_bytes=ALIGN),
                    tail.tile([P, N, PACK], BF16, name="x2_woven1", offset=0, align_bytes=ALIGN)]

        def pick_late_companions(n0, n1, tag):
            rows = keep.tile([P, PACK, n1 - n0], BF16, name=f"x2_late{n0}", tag=tag, align_bytes=ALIGN)
            for t in range(PACK):
                nc.vector.tensor_copy(out=rows[:, t, :], in_=h[1][t][:].indirect(p2[:, n0 // PER_COLUMN:n1 // PER_COLUMN]))
            weave_on_scalar(x2_woven[1], rows, n0, 0)

        weave_on_scalar(x2_woven[0], x2_rows, 0, 0)
        x1_q = [quantise(x1_woven[0], "x1q0", "x1q0")]
        pick_late_companions(0, LATE_SPLIT, "gain1")
        x1_q.append(quantise(x1_woven[1], "x1q1", "x1q1"))
        pick_late_companions(LATE_SPLIT, N, "x1_woven1")
        x2_q = [quantise(x2_woven[0], "x2q0", "x2q0")]

        def score_pass(bank, m, a, x_q):
            nc.tensor.matmul_mx(out=bank[:], lhsT=v2_w[:, a, m * P:(m + 1) * P].bitcast(FP8X4),
                                lhsT_scale=v2_s[4 * a:P, m * P:(m + 1) * P], rhs=x_q[0][:].bitcast(FP8X4), rhs_scale=x_q[1][:],
                                start=(a == 0), stop=(a == BLOCKS - 1))

        e1 = [bank_tile(TILES + m, f"e1_{m}") for m in range(TILES)]
        e2 = [bank_tile(m, f"e2_{m}") for m in range(TILES)]
        for a in range(BLOCKS):
            for m in range(TILES):
                score_pass(e1[m], m, a, x1_q[a])
        for m in range(TILES):
            score_pass(e2[m], m, 0, x2_q[0])

        def shift(m, tile):
            nc.vector.tensor_tensor(out=tile[:], in0=e1[m][:], in1=exc_sb[:, m, :], op=ALU.add)
            return tile

        last = TILES - 1
        result = [shift(0, keep.tile([P, N], F32, name="result0")),
                  shift(1, keep.tile([P, N], F32, name="result1", tag="bent_last", align_bytes=ALIGN))]
        x2_q.append(quantise(x2_woven[1], "x2q1", "x2q1"))
        e1_last = keep.tile([P, N], F32, name="e1_last")
        nc.scalar.copy(out=e1_last[:], in_=e1[last][:])
        result.append(shift(2, tail.tile([P, N], F32, name="result2", offset=0, align_bytes=ALIGN)))
        result.append(tail.tile([P, N], F32, name="result3", offset=4 * N, align_bytes=ALIGN))
        nc.gpsimd.tensor_tensor(out=result[last][:], in0=e1_last[:], in1=exc_sb[:, last, :], op=ALU.add)
        for m in range(TILES):
            score_pass(e2[m], m, 1, x2_q[1])
        for m in range(TILES):
            nc.vector.tensor_tensor(out=result[m][:], in0=e2[m][:], in1=result[m][:], op=ALU.mult)
            nc.sync.dma_start(out=out[m * P:(m + 1) * P, :], in_=result[m][:])
